import numpy as np
import ml_dtypes


def mxq(x, axis, fmt="e4m3"):
    dtype, down = {"e4m3": (ml_dtypes.float8_e4m3fn, 7), "e5m2": (ml_dtypes.float8_e5m2, 14)}[fmt]
    v = np.moveaxis(np.asarray(x, np.float32).astype(ml_dtypes.bfloat16).astype(np.float64), axis, -1)
    blocks = v.reshape(v.shape[:-1] + (-1, 32))
    amax = np.abs(blocks).max(-1, keepdims=True)
    byte = np.maximum(np.where(amax > 0, np.frexp(amax)[1] - 1 + 127, 0) - down, 1)
    scale = np.exp2(byte - 127.0)
    codes = (blocks / scale).astype(np.float32).astype(dtype).astype(np.float64)
    return np.moveaxis((codes * scale).reshape(v.shape), -1, axis)


WIDE = False


def mx_kscale(k):
    if not WIDE:
        return np.ones(k)
    levels = np.array([10, -10, 5, -5, 0])
    if k % 512:
        return np.exp2(np.random.permutation(np.resize(levels, k // 32))).repeat(32)
    a = np.empty((k // 512, 16))
    for p in range(k // 512):
        a[p, :8] = np.random.permutation(np.resize(levels, 8))
        for g in range(8):
            far = levels[np.abs(levels - a[p, g]) >= 10]
            a[p, g + 8] = far[np.random.randint(len(far))]
    return np.exp2(a.ravel()).repeat(32)


def f64(x):
    return np.asarray(x).astype(np.float64)


def striped(idx):
    return np.tile(idx.reshape(-1, 16).T, (8, 1)).astype(np.uint16)


def unstriped(offs):
    return offs[:16].T.reshape(-1).astype(np.int64)


def pack_weight(w):
    k, n = w.shape
    w = f64(np.asarray(w, np.float32).astype(ml_dtypes.bfloat16)).reshape(k // 32, 32, n)
    amax = np.abs(w).max(1)
    byte = np.clip(np.where(amax > 0, np.frexp(amax)[1] - 1 + 127 - 7, 1), 1, 254)
    scaled = (w * np.exp2(127.0 - byte)[:, None, :]).reshape(k, n).astype(np.float32)
    words = np.ascontiguousarray(scaled.reshape(k // 512, 128, 4, n).transpose(0, 1, 3, 2)).astype(ml_dtypes.float8_e4m3fn).view(np.uint8)
    return words, np.ascontiguousarray(byte.astype(np.uint8).reshape(k // 512, 16, n))


def unpack_weight(words, scales):
    g, p, n, _ = words.shape
    vals = np.ascontiguousarray(words).view(ml_dtypes.float8_e4m3fn).astype(np.float64) * np.repeat(np.exp2(scales.astype(np.float64) - 127.0), 8, axis=1)[..., None]
    return vals.transpose(0, 1, 3, 2).reshape(g * 512, n)


E2M1 = np.array([0.0, 0.5, 1.0, 1.5, 2.0, 3.0, 4.0, 6.0, -0.0, -0.5, -1.0, -1.5, -2.0, -3.0, -4.0, -6.0])


def pack_fp4(w):
    k, n = w.shape
    w = f64(np.asarray(w, np.float32).astype(ml_dtypes.bfloat16)).reshape(k // 32, 32, n)
    amax = np.abs(w).max(1)
    mant, ex = np.frexp(amax / 6.0)
    byte = np.clip(np.where(amax > 0, np.where(mant > 0.5, ex, ex - 1) + 127, 1), 1, 254)
    scaled = (w * np.exp2(127.0 - byte)[:, None, :]).reshape(k, n).astype(np.float32)
    c = np.ascontiguousarray(scaled.reshape(k // 512, 128, 4, n).transpose(0, 1, 3, 2)).astype(ml_dtypes.float4_e2m1fn).view(np.uint8) & 0xF
    words = (c[..., 0::2] | (c[..., 1::2] << 4)).reshape(k // 512, 128, 2 * n)
    return np.ascontiguousarray(words), np.ascontiguousarray(byte.astype(np.uint8).reshape(k // 512, 16, n))


def unpack_fp4(words, scales):
    g, _, n = scales.shape
    words = np.ascontiguousarray(words).reshape(g, 128, n, 2)
    nib = np.empty((g, 128, n, 4), np.uint8)
    nib[..., 0::2] = words & 0xF
    nib[..., 1::2] = words >> 4
    vals = E2M1[nib] * np.repeat(np.exp2(scales.astype(np.float64) - 127.0), 8, axis=1)[..., None]
    return vals.transpose(0, 1, 3, 2).reshape(g * 512, n)


def relu(v):
    return np.maximum(v, 0.0)


K, T, S, H, N = 1024, 2048, 1024, 512, 128
P = 2 ** 7


def setup_inputs():
    n = np.random.standard_normal
    s = mx_kscale(K)[:, None]
    u = mx_kscale(H)
    packed_xT = pack_weight(n((K, T)) * s)
    packed_w2 = pack_fp4(n((H, N)) / np.sqrt(H) / u[:, None])
    return {
        "x_words": packed_xT[0],
        "x_scales": packed_xT[1],
        "w1": (n((K, H)) / np.sqrt(K) / s * u).astype(np.float32),
        "w2_words": packed_w2[0],
        "w2_scales": packed_w2[1],
        "share": np.tile(np.random.uniform(0.1, 0.9, S), (P, 1)).astype(np.float32),
        "offs": striped(np.random.permutation(T)[:S]),
        "par": striped(np.random.permutation(S)[(S * np.random.uniform(0, 1, S) ** 4).astype(np.int64)]),
    }


def reference(x_words, x_scales, w1, w2_words, w2_scales, share, offs, par):
    xq = unpack_weight(x_words, x_scales)[:, unstriped(offs)]
    h = relu(mxq(f64(w1), 0, "e4m3").T @ xq)
    z = h + h[:, unstriped(par)] * f64(share)[:1]
    return unpack_fp4(w2_words, w2_scales).T @ mxq(z, 0, "e4m3")

@@ -1,0 +1,238 @@
+from contextlib import ExitStack
+
+import concourse.mybir as mybir
+from concourse.masks import make_identity
+
+K, T, S, H, N = 1024, 2048, 1024, 512, 128
+FLOPS = 2 * K * H * S + 2 * H * N * S
+
+F32 = mybir.dt.float32
+BF16 = mybir.dt.bfloat16
+I32 = mybir.dt.int32
+U32 = mybir.dt.uint32
+U16 = mybir.dt.uint16
+U8 = mybir.dt.uint8
+FP8X4 = mybir.dt.float8_e4m3fn_x4
+FP4X4 = mybir.dt.float4_e2m1fn_x4
+ACT = mybir.ActivationFunctionType
+MULT = mybir.AluOpType.mult
+ADD = mybir.AluOpType.add
+
+P = 128
+PASSES = K // 512
+HALF = 512
+TILES = H // P
+
+
+def tile_picked_treeup_relu_p_kernel(
+    tc, x_words, x_scales, w1, w2_words, w2_scales, share, offs, par, out
+):
+    nc = tc.nc
+    with ExitStack() as ctx:
+        keep = ctx.enter_context(tc.tile_pool(name="keep", bufs=1))
+        reuse = ctx.enter_context(tc.tile_pool(name="reuse", bufs=1))
+        acc_pool = ctx.enter_context(tc.psum_pool(name="acc", bufs=2))
+        sum_pool = ctx.enter_context(tc.psum_pool(name="sums", bufs=4))
+        back_pool = ctx.enter_context(tc.psum_pool(name="back", bufs=2))
+
+        offs_sb = keep.tile([P, S // 16], U16, name="offs_sb")
+        par_sb = keep.tile([P, S // 16], U16, name="par_sb")
+        xs_all = keep.tile([P, T], U8, name="xs_all", align_bytes=64)
+        w2_sc = keep.tile([P, N], U8, name="w2_sc", align_bytes=64)
+        w2_cd = keep.tile([P, 2 * N], U8, name="w2_cd", align_bytes=64)
+        nc.gpsimd.memset(xs_all[:].bitcast(I32), 0)
+        nc.vector.memset(w2_sc[:].bitcast(I32), 0)
+        ident = keep.tile([P, P], F32, name="ident")
+        make_identity(nc, ident[:])
+        ident_bf = ident
+
+        share_col = keep.tile([P, 2, 4], F32, name="share_col")
+        nc.sync.dma_start(offs_sb[:], offs)
+        nc.sync.dma_start(share_col[:], share[0, :].rearrange("(b p a) -> p b a", b=2, a=4))
+        nc.sync.dma_start(par_sb[:], par)
+        for q in range(4):
+            nc.sync.dma_start(
+                xs_all[32 * q : 32 * q + 8, :].bitcast(I32),
+                x_scales[:, 4 * q : 4 * q + 4, :].bitcast(I32),
+            )
+        xw_all = {}
+        w_raw = {}
+
+        def load_x(z):
+            xw_all[z] = keep.tile([P, T], I32, name=f"xw_all{z}", align_bytes=64)
+            nc.sync.dma_start(xw_all[z][:], x_words[z].rearrange("p n t -> p (n t)").bitcast(I32))
+
+        def load_w1(c):
+            for z in range(PASSES):
+                if c == TILES - 1:
+                    t = reuse.tile([P, 4, P], F32, name=f"w_raw{c}_{z}", offset=(1536, 7168)[z])
+                else:
+                    t = keep.tile([P, 4, P], F32, name=f"w_raw{c}_{z}", align_bytes=64)
+                nc.sync.dma_start(
+                    t[:], w1[512 * z : 512 * (z + 1), c * P : (c + 1) * P].rearrange("(p j) c -> p j c", j=4)
+                )
+                w_raw[c, z] = t[:]
+
+        load_x(0)
+        load_w1(0)
+        load_x(1)
+        for c in range(1, TILES):
+            load_w1(c)
+        nc.sync.dma_start(w2_cd[:].bitcast(I32), w2_words[0].bitcast(I32))
+        for q in range(4):
+            nc.sync.dma_start(
+                w2_sc[32 * q : 32 * q + 4, :].bitcast(I32), w2_scales[0, 4 * q : 4 * q + 4, :].bitcast(I32)
+            )
+
+        share_sb = keep.tile([P, S], F32, name="share_sb")
+        for b in range(2):
+            bank = back_pool.tile([P, 4, P], F32, name="back")
+            for a in range(4):
+                nc.tensor.transpose(bank[:, a, :], share_col[:, b, a : a + 1].to_broadcast([P, P]), ident[:])
+            nc.scalar.activation(
+                share_sb[:, HALF * b : HALF * (b + 1)].rearrange("p (n a) -> p n a", a=4),
+                bank[:].rearrange("p a n -> p n a"),
+                ACT.Copy,
+            )
+
+        xs = keep.tile([P, S], U8, name="xs", align_bytes=64)
+        nc.vector.tensor_copy(xs[:], xs_all[:].indirect(offs_sb[:]))
+        xw = [keep.tile([P, S], U32, name=f"xw{z}", align_bytes=64) for z in range(PASSES)]
+        nc.vector.tensor_copy(xw[0][:], xw_all[0][:].bitcast(U32).indirect(offs_sb[:]))
+        for b in range(2):
+            nc.vector.tensor_copy(
+                xw[1][:, HALF * b : HALF * (b + 1)],
+                xw_all[1][:].bitcast(U32).indirect(offs_sb[:, 32 * b : 32 * (b + 1)]),
+            )
+
+        h = [keep.tile([P, S], F32, name=f"h{c}") for c in range(TILES)]
+
+        w_q = {}
+
+        def quantise_w1(c):
+            grouped = keep.tile([P, PASSES, P, 4], BF16, name=f"w_grp{c}", tag=f"w_grp{c}", align_bytes=64)
+            for z in range(PASSES):
+                dst = grouped[:, z, :, :].rearrange("p (c i) t -> p c t i", i=4)
+                src = w_raw[c, z].rearrange("p t (c i) -> p c t i", i=4)
+                if c in [1]:
+                    nc.vector.tensor_copy(dst, src)
+                else:
+                    nc.scalar.copy(dst, src)
+            codes = keep.tile([P, PASSES * P], U32, name=f"w_cd{c}", align_bytes=64)
+            scales = keep.tile([P, PASSES * P], U8, name=f"w_sc{c}", align_bytes=64)
+            nc.vector.quantize_mx(
+                out=codes[:].bitcast(FP8X4), scales=scales[:], in_=grouped[:].rearrange("p z c t -> p (z c t)")
+            )
+            w_q[c] = codes, scales
+
+        def first_layer(c):
+            codes, scales = w_q[c]
+            for b in range(2):
+                cols = slice(HALF * b, HALF * (b + 1))
+                acc = acc_pool.tile([P, HALF], F32, name="acc")
+                for z in range(PASSES):
+                    nc.tensor.matmul_mx(
+                        out=acc[:],
+                        lhsT=codes[:, z * P : (z + 1) * P].bitcast(FP8X4),
+                        lhsT_scale=scales[:, z * P : (z + 1) * P],
+                        rhs=xw[z][:, cols].bitcast(FP8X4),
+                        rhs_scale=xs[4 * z : P, cols],
+                        start=(z == 0),
+                        stop=(z == PASSES - 1),
+                    )
+                nc.scalar.activation(h[c][:, cols], acc[:], ACT.Relu)
+
+        chunks = [(0, 256), (256, 512), (512, 768), (768, 1024)]
+        z_t = {}
+        for j0, j1 in chunks:
+            z_t[j0] = reuse.tile([P, (j1 - j0) // P, 2, P, 2], BF16, name=f"z_t{j0}", offset=(j0 * 8 + 4096) % 8192)
+
+        def influence(c, j0, j1, add_on_vector=False):
+            n = j1 - j0
+            if (c, j0) == (1, 512):
+                taken = reuse.tile([P, n], F32, name="taken1_512", offset=8192)
+            else:
+                slot = {(0, 0): "w_raw1_1", (0, 512): "w_raw2_1", (2, 512): "taken3_0", (2, 768): "taken3_512"}.get((c, j0), f"taken{c}_{j0}")
+                taken = keep.tile([P, n], F32, name=f"taken{c}_{j0}", tag=slot, align_bytes=64)
+            nc.vector.tensor_tensor(
+                taken[:], h[c][:].indirect(par_sb[:, j0 // 16 : j1 // 16]), share_sb[:, j0:j1], MULT
+            )
+            if add_on_vector:
+                z_nat = keep.tile([P, n], BF16, name=f"z_nat{c}_{j0}")
+                nc.vector.tensor_tensor(z_nat[:], h[c][:, j0:j1], taken[:], ADD)
+                bank = sum_pool.tile([P, n // P, P], BF16, name="sums")
+                for b in range(n // P):
+                    nc.tensor.transpose(bank[:, b, :], z_nat[:, b * P : (b + 1) * P], ident_bf[:])
+            else:
+                bank = sum_pool.tile([P, n // P, P], F32, name="sums")
+                for b in range(n // P):
+                    nc.tensor.matmul(
+                        bank[:, b, :], h[c][:, j0 + b * P : j0 + (b + 1) * P], ident[:],
+                        start=(b == 0), stop=False, is_transpose=True,
+                    )
+                for b in range(n // P):
+                    nc.tensor.matmul(
+                        bank[:, b, :], taken[:, b * P : (b + 1) * P], ident[:],
+                        start=False, stop=(b == n // P - 1), is_transpose=True,
+                    )
+            for a0, a1 in chunks:
+                if j0 <= a0 and a1 <= j1:
+                    nc.scalar.copy(
+                        z_t[a0][:, :, :, 32 * c : 32 * (c + 1), :],
+                        bank[:, (a0 - j0) // P : (a1 - j0) // P, :].rearrange("j b (p u e) -> j b u p e", u=2, e=2),
+                    )
+
+        def second_layer(j0, j1, on_vector, out_on_vector):
+            n = j1 - j0
+            words = z_t[j0][:].rearrange("j b u p e -> j (b u p e)").bitcast(F32)
+            grouped = keep.tile([P, n * 4], BF16, name=f"z_grp{j0}", align_bytes=64)
+            for b0 in range(0, n // P, 2):
+                nb = min(2, n // P - b0)
+                bank = back_pool.tile([P, nb, 2, P], F32, name="back")
+                for b in range(nb):
+                    for u in range(2):
+                        w0 = ((b0 + b) * 2 + u) * P
+                        nc.tensor.transpose(bank[:, b, u, :], words[:, w0 : w0 + P], ident[:])
+                dst = grouped[:, b0 * 4 * P : (b0 + nb) * 4 * P].bitcast(F32).rearrange("p (b j u) -> p b j u", b=nb, u=2)
+                src = bank[:].rearrange("p b u j -> p b j u")
+                if on_vector:
+                    nc.vector.tensor_copy(dst, src)
+                else:
+                    nc.scalar.copy(dst, src)
+            codes = keep.tile([P, n], U32, name=f"z_cd{j0}", align_bytes=64)
+            scales = keep.tile([P, n], U8, name=f"z_sc{j0}", align_bytes=64)
+            nc.vector.quantize_mx(out=codes[:].bitcast(FP8X4), scales=scales[:], in_=grouped[:])
+            res = acc_pool.tile([P, n], F32, name="acc")
+            nc.tensor.matmul_mx(
+                out=res[:], lhsT=w2_cd[:].bitcast(FP4X4), lhsT_scale=w2_sc[:],
+                rhs=codes[:].bitcast(FP8X4), rhs_scale=scales[:], start=True, stop=True,
+            )
+            res_sb = keep.tile([P, n], F32, name=f"res_sb{j0}")
+            if out_on_vector:
+                nc.vector.tensor_copy(res_sb[:], res[:])
+            else:
+                nc.scalar.copy(res_sb[:], res[:])
+            nc.sync.dma_start(out[:, j0:j1], res_sb[:])
+
+        quantise_w1(0)
+        first_layer(0)
+        quantise_w1(1)
+        quantise_w1(2)
+        first_layer(1)
+        quantise_w1(3)
+        first_layer(2)
+        first_layer(3)
+        influence(0, 0, 512)
+        influence(0, 512, 1024)
+        influence(1, 0, 512)
+        influence(1, 512, 1024)
+        influence(2, 0, 512)
+        influence(3, 0, 512)
+        second_layer(0, 256, False, False)
+        second_layer(256, 512, False, False)
+        influence(3, 512, 768)
+        influence(3, 768, 1024)
+        influence(2, 512, 768)
+        influence(2, 768, 1024)
+        second_layer(512, 768, True, False)
+        second_layer(768, 1024, True, True)

@@ -16,7 +16,6 @@ FP8X4 = mybir.dt.float8_e4m3fn_x4
 FP4X4 = mybir.dt.float4_e2m1fn_x4
 ACT = mybir.ActivationFunctionType
 MULT = mybir.AluOpType.mult
-ADD = mybir.AluOpType.add
 
 P = 128
 PASSES = K // 512
@@ -30,63 +29,57 @@ def tile_picked_treeup_relu_p_kernel(
     nc = tc.nc
     with ExitStack() as ctx:
         keep = ctx.enter_context(tc.tile_pool(name="keep", bufs=1))
+        psum = ctx.enter_context(tc.psum_pool(name="psum", bufs=1))
+        reuses = {"xw1_1":"w_raw0_0","w_grp1_0":"w_raw0_1","w_grp2_0":"w_cd0_1","taken0_512":"w_raw2_1","taken1_512":"w_raw3_1","z_t0":"w_raw3_0"}
+
+        placed = {"xw_all0":0,"w_grp0_0":0,"w_grp0_1":1024,"z_t512":8192,"z_t768":10240,"w_grp3_0":9216,"w_cd1_0":9216,"taken3_0":12288,"taken2_512":12288,"taken2_768":13312}
         reuse = ctx.enter_context(tc.tile_pool(name="reuse", bufs=1))
-        acc_pool = ctx.enter_context(tc.psum_pool(name="acc", bufs=2))
-        sum_pool = ctx.enter_context(tc.psum_pool(name="sums", bufs=4))
-        back_pool = ctx.enter_context(tc.psum_pool(name="back", bufs=2))
+
+        def sbuf(name, shape, dtype):
+            if name in placed:
+                return reuse.tile(shape, dtype, name=name, offset=placed[name], align_bytes=64)
+            return keep.tile(shape, dtype, name=name, tag=reuses.get(name, name), align_bytes=64)
 
         offs_sb = keep.tile([P, S // 16], U16, name="offs_sb")
         par_sb = keep.tile([P, S // 16], U16, name="par_sb")
-        xs_all = keep.tile([P, T], U8, name="xs_all", align_bytes=64)
-        w2_sc = keep.tile([P, N], U8, name="w2_sc", align_bytes=64)
-        w2_cd = keep.tile([P, 2 * N], U8, name="w2_cd", align_bytes=64)
+        xs_all = sbuf("xs_all", [P, T], U8)
+        w2_sc = sbuf("w2_sc", [P, N], U8)
+        w2_cd = sbuf("w2_cd", [P, 2 * N], U8)
         nc.gpsimd.memset(xs_all[:].bitcast(I32), 0)
         nc.vector.memset(w2_sc[:].bitcast(I32), 0)
-        ident = keep.tile([P, P], F32, name="ident")
+        ident = sbuf("ident", [P, P], F32)
         make_identity(nc, ident[:])
-        ident_bf = ident
 
-        share_col = keep.tile([P, 2, 4], F32, name="share_col")
+        share_col = sbuf("share_col", [P, 2, 4], F32)
         nc.sync.dma_start(offs_sb[:], offs)
-        nc.sync.dma_start(share_col[:], share[0, :].rearrange("(b p a) -> p b a", b=2, a=4))
         nc.sync.dma_start(par_sb[:], par)
+        nc.scalar.dma_start(share_col[:], share[0, :].rearrange("(b p a) -> p b a", b=2, a=4))
         for q in range(4):
             nc.sync.dma_start(
                 xs_all[32 * q : 32 * q + 8, :].bitcast(I32),
                 x_scales[:, 4 * q : 4 * q + 4, :].bitcast(I32),
             )
-        xw_all = {}
-        w_raw = {}
-
-        def load_x(z):
-            xw_all[z] = keep.tile([P, T], I32, name=f"xw_all{z}", align_bytes=64)
+        xw_all = []
+        for z in range(PASSES):
+            xw_all.append(sbuf(f"xw_all{z}", [P, T], I32))
             nc.sync.dma_start(xw_all[z][:], x_words[z].rearrange("p n t -> p (n t)").bitcast(I32))
-
-        def load_w1(c):
-            for z in range(PASSES):
-                if c == TILES - 1:
-                    t = reuse.tile([P, 4, P], F32, name=f"w_raw{c}_{z}", offset=(1536, 7168)[z])
-                else:
-                    t = keep.tile([P, 4, P], F32, name=f"w_raw{c}_{z}", align_bytes=64)
-                nc.sync.dma_start(
-                    t[:], w1[512 * z : 512 * (z + 1), c * P : (c + 1) * P].rearrange("(p j) c -> p j c", j=4)
-                )
-                w_raw[c, z] = t[:]
-
-        load_x(0)
-        load_w1(0)
-        load_x(1)
-        for c in range(1, TILES):
-            load_w1(c)
+        w_raw = {}
+        for z, c0, c1 in [(0, 0, 1), (1, 0, 1), (0, 1, 2), (1, 1, 2), (0, 2, 3), (1, 2, 3), (0, 3, 4), (1, 3, 4)]:
+            t = sbuf(f"w_raw{c0}_{z}", [P, 4, (c1 - c0) * P], F32)
+            nc.sync.dma_start(
+                t[:], w1[512 * z : 512 * (z + 1), c0 * P : c1 * P].rearrange("(p j) c -> p j c", j=4)
+            )
+            for c in range(c0, c1):
+                w_raw[c, z] = t[:, :, (c - c0) * P : (c - c0 + 1) * P]
         nc.sync.dma_start(w2_cd[:].bitcast(I32), w2_words[0].bitcast(I32))
         for q in range(4):
             nc.sync.dma_start(
                 w2_sc[32 * q : 32 * q + 4, :].bitcast(I32), w2_scales[0, 4 * q : 4 * q + 4, :].bitcast(I32)
             )
 
-        share_sb = keep.tile([P, S], F32, name="share_sb")
+        share_sb = sbuf("share_sb", [P, S], F32)
         for b in range(2):
-            bank = back_pool.tile([P, 4, P], F32, name="back")
+            bank = psum.tile([P, 4, P], F32, name="spread", tag=f"bank{6 + b}")
             for a in range(4):
                 nc.tensor.transpose(bank[:, a, :], share_col[:, b, a : a + 1].to_broadcast([P, P]), ident[:])
             nc.scalar.activation(
@@ -95,144 +88,245 @@ def tile_picked_treeup_relu_p_kernel(
                 ACT.Copy,
             )
 
-        xs = keep.tile([P, S], U8, name="xs", align_bytes=64)
-        nc.vector.tensor_copy(xs[:], xs_all[:].indirect(offs_sb[:]))
-        xw = [keep.tile([P, S], U32, name=f"xw{z}", align_bytes=64) for z in range(PASSES)]
-        nc.vector.tensor_copy(xw[0][:], xw_all[0][:].bitcast(U32).indirect(offs_sb[:]))
-        for b in range(2):
-            nc.vector.tensor_copy(
-                xw[1][:, HALF * b : HALF * (b + 1)],
-                xw_all[1][:].bitcast(U32).indirect(offs_sb[:, 32 * b : 32 * (b + 1)]),
-            )
-
-        h = [keep.tile([P, S], F32, name=f"h{c}") for c in range(TILES)]
-
+        xs = sbuf("xs", [P, S], U8)
+        xw = {}
         w_q = {}
+        h = [sbuf(f"h{c}", [P, S], F32) for c in range(TILES)]
 
-        def quantise_w1(c):
-            grouped = keep.tile([P, PASSES, P, 4], BF16, name=f"w_grp{c}", tag=f"w_grp{c}", align_bytes=64)
-            for z in range(PASSES):
-                dst = grouped[:, z, :, :].rearrange("p (c i) t -> p c t i", i=4)
-                src = w_raw[c, z].rearrange("p t (c i) -> p c t i", i=4)
-                if c in [1]:
-                    nc.vector.tensor_copy(dst, src)
-                else:
-                    nc.scalar.copy(dst, src)
-            codes = keep.tile([P, PASSES * P], U32, name=f"w_cd{c}", align_bytes=64)
-            scales = keep.tile([P, PASSES * P], U8, name=f"w_sc{c}", align_bytes=64)
+        def pick_words(z, b0, b1):
+            t = sbuf(f"xw{z}_{b0}", [P, HALF * (b1 - b0)], U32)
+            nc.vector.tensor_copy(t[:], xw_all[z][:].bitcast(U32).indirect(offs_sb[:, 32 * b0 : 32 * b1]))
+            for b in range(b0, b1):
+                xw[z, b] = t[:, HALF * (b - b0) : HALF * (b - b0 + 1)]
+
+        w_grp = {}
+
+        def round_w1(c, z, on_vector):
+            z0 = z if c == 0 else 0
+            if z == z0:
+                w_grp[c, z0] = sbuf(f"w_grp{c}_{z0}", [P, 1 if c == 0 else PASSES, P, 4], BF16)
+            dst = w_grp[c, z0][:, z - z0, :, :].rearrange("p (c i) t -> p c t i", i=4)
+            src = w_raw[c, z].rearrange("p t (c i) -> p c t i", i=4)
+            if on_vector:
+                nc.vector.tensor_copy(dst, src)
+            else:
+                nc.scalar.copy(dst, src)
+
+        def quantise_w1(c, z0):
+            passes = 1 if c == 0 else PASSES
+            codes = sbuf(f"w_cd{c}_{z0}", [P, passes * P], U32)
+            scales = sbuf(f"w_sc{c}_{z0}", [P, passes * P], U8)
             nc.vector.quantize_mx(
-                out=codes[:].bitcast(FP8X4), scales=scales[:], in_=grouped[:].rearrange("p z c t -> p (z c t)")
+                out=codes[:].bitcast(FP8X4), scales=scales[:], in_=w_grp[c, z0][:].rearrange("p z c t -> p (z c t)")
             )
-            w_q[c] = codes, scales
+            for z in range(passes):
+                w_q[c, z0 + z] = codes[:, z * P : (z + 1) * P], scales[:, z * P : (z + 1) * P]
 
-        def first_layer(c):
-            codes, scales = w_q[c]
-            for b in range(2):
-                cols = slice(HALF * b, HALF * (b + 1))
-                acc = acc_pool.tile([P, HALF], F32, name="acc")
-                for z in range(PASSES):
-                    nc.tensor.matmul_mx(
-                        out=acc[:],
-                        lhsT=codes[:, z * P : (z + 1) * P].bitcast(FP8X4),
-                        lhsT_scale=scales[:, z * P : (z + 1) * P],
-                        rhs=xw[z][:, cols].bitcast(FP8X4),
-                        rhs_scale=xs[4 * z : P, cols],
-                        start=(z == 0),
-                        stop=(z == PASSES - 1),
-                    )
-                nc.scalar.activation(h[c][:, cols], acc[:], ACT.Relu)
+        accs = {}
 
-        chunks = [(0, 256), (256, 512), (512, 768), (768, 1024)]
+        def product(c, z, b, bank=None):
+            if z == 0:
+                accs[c, b] = psum.tile([P, HALF], F32, name="acc", tag=f"bank{bank}")
+            cols = slice(HALF * b, HALF * (b + 1))
+            nc.tensor.matmul_mx(
+                out=accs[c, b][:],
+                lhsT=w_q[c, z][0].bitcast(FP8X4),
+                lhsT_scale=w_q[c, z][1],
+                rhs=xw[z, b].bitcast(FP8X4),
+                rhs_scale=xs[4 * z : P, cols],
+                start=(z == 0),
+                stop=(z == PASSES - 1),
+            )
+
+        def relu(c, b, on_vector=False):
+            cols = slice(HALF * b, HALF * (b + 1))
+            if on_vector:
+                nc.vector.tensor_scalar(h[c][:, cols], accs[c, b][:], 0.0, None, op0=mybir.AluOpType.max)
+            else:
+                nc.scalar.activation(h[c][:, cols], accs[c, b][:], ACT.Relu)
+
+        chunks = [(0,512), (512,768), (768,1024)]
         z_t = {}
         for j0, j1 in chunks:
-            z_t[j0] = reuse.tile([P, (j1 - j0) // P, 2, P, 2], BF16, name=f"z_t{j0}", offset=(j0 * 8 + 4096) % 8192)
+            z_t[j0] = sbuf(f"z_t{j0}", [P, (j1 - j0) // P, 2, P, 2], BF16)
 
-        def influence(c, j0, j1, add_on_vector=False):
-            n = j1 - j0
-            if (c, j0) == (1, 512):
-                taken = reuse.tile([P, n], F32, name="taken1_512", offset=8192)
+        taken = {}
+        sums = {}
+
+        def copy(on_vector, dst, src):
+            if on_vector:
+                nc.vector.tensor_copy(dst, src)
             else:
-                slot = {(0, 0): "w_raw1_1", (0, 512): "w_raw2_1", (2, 512): "taken3_0", (2, 768): "taken3_512"}.get((c, j0), f"taken{c}_{j0}")
-                taken = keep.tile([P, n], F32, name=f"taken{c}_{j0}", tag=slot, align_bytes=64)
+                nc.scalar.copy(dst, src)
+
+        def gather(c, j0, j1):
+            taken[c, j0] = sbuf(f"taken{c}_{j0}", [P, j1 - j0], F32)
             nc.vector.tensor_tensor(
-                taken[:], h[c][:].indirect(par_sb[:, j0 // 16 : j1 // 16]), share_sb[:, j0:j1], MULT
+                taken[c, j0][:], h[c][:].indirect(par_sb[:, j0 // 16 : j1 // 16]), share_sb[:, j0:j1], MULT
             )
-            if add_on_vector:
-                z_nat = keep.tile([P, n], BF16, name=f"z_nat{c}_{j0}")
-                nc.vector.tensor_tensor(z_nat[:], h[c][:, j0:j1], taken[:], ADD)
-                bank = sum_pool.tile([P, n // P, P], BF16, name="sums")
-                for b in range(n // P):
-                    nc.tensor.transpose(bank[:, b, :], z_nat[:, b * P : (b + 1) * P], ident_bf[:])
-            else:
-                bank = sum_pool.tile([P, n // P, P], F32, name="sums")
-                for b in range(n // P):
-                    nc.tensor.matmul(
-                        bank[:, b, :], h[c][:, j0 + b * P : j0 + (b + 1) * P], ident[:],
-                        start=(b == 0), stop=False, is_transpose=True,
-                    )
-                for b in range(n // P):
-                    nc.tensor.matmul(
-                        bank[:, b, :], taken[:, b * P : (b + 1) * P], ident[:],
-                        start=False, stop=(b == n // P - 1), is_transpose=True,
-                    )
+
+        def turn_h(c, j0, j1, bank):
+            sums[c, j0] = psum.tile([P, (j1 - j0) // P, P], F32, name="sums", tag=f"bank{bank}")
+            for b in range((j1 - j0) // P):
+                nc.tensor.matmul(
+                    sums[c, j0][:, b, :], h[c][:, j0 + b * P : j0 + (b + 1) * P], ident[:],
+                    start=(b == 0), stop=False, is_transpose=True,
+                )
+
+        def turn_taken(c, j0, j1):
+            h0 = j0 // HALF * HALF
+            for b in range((j1 - j0) // P):
+                nc.tensor.matmul(
+                    sums[c, h0][:, (j0 - h0) // P + b, :], taken[c, j0][:, b * P : (b + 1) * P], ident[:],
+                    start=False, stop=(j0 + (b + 1) * P == h0 + HALF), is_transpose=True,
+                )
+
+        def round_z(c, j0, j1, on_vector=False):
             for a0, a1 in chunks:
                 if j0 <= a0 and a1 <= j1:
-                    nc.scalar.copy(
+                    copy(
+                        on_vector,
                         z_t[a0][:, :, :, 32 * c : 32 * (c + 1), :],
-                        bank[:, (a0 - j0) // P : (a1 - j0) // P, :].rearrange("j b (p u e) -> j b u p e", u=2, e=2),
+                        sums[c, j0][:, (a0 - j0) // P : (a1 - j0) // P, :].rearrange("j b (p u e) -> j b u p e", u=2, e=2),
                     )
 
-        def second_layer(j0, j1, on_vector, out_on_vector):
-            n = j1 - j0
+        z_grp = {}
+        backs = {}
+
+        def turn_back(j0, j1, b0, nb, bank):
             words = z_t[j0][:].rearrange("j b u p e -> j (b u p e)").bitcast(F32)
-            grouped = keep.tile([P, n * 4], BF16, name=f"z_grp{j0}", align_bytes=64)
-            for b0 in range(0, n // P, 2):
-                nb = min(2, n // P - b0)
-                bank = back_pool.tile([P, nb, 2, P], F32, name="back")
-                for b in range(nb):
-                    for u in range(2):
-                        w0 = ((b0 + b) * 2 + u) * P
-                        nc.tensor.transpose(bank[:, b, u, :], words[:, w0 : w0 + P], ident[:])
-                dst = grouped[:, b0 * 4 * P : (b0 + nb) * 4 * P].bitcast(F32).rearrange("p (b j u) -> p b j u", b=nb, u=2)
-                src = bank[:].rearrange("p b u j -> p b j u")
-                if on_vector:
-                    nc.vector.tensor_copy(dst, src)
-                else:
-                    nc.scalar.copy(dst, src)
-            codes = keep.tile([P, n], U32, name=f"z_cd{j0}", align_bytes=64)
-            scales = keep.tile([P, n], U8, name=f"z_sc{j0}", align_bytes=64)
-            nc.vector.quantize_mx(out=codes[:].bitcast(FP8X4), scales=scales[:], in_=grouped[:])
-            res = acc_pool.tile([P, n], F32, name="acc")
+            backs[j0, b0] = psum.tile([P, nb, 2, P], F32, name="back", tag=f"bank{bank}")
+            for b in range(nb):
+                for u in range(2):
+                    w0 = ((b0 + b) * 2 + u) * P
+                    nc.tensor.transpose(backs[j0, b0][:, b, u, :], words[:, w0 : w0 + P], ident[:])
+
+        def weave(j0, j1, b0, nb, on_vector):
+            if b0 == 0:
+                z_grp[j0] = sbuf(f"z_grp{j0}", [P, (j1 - j0) * 4], BF16)
+            dst = z_grp[j0][:, b0 * 4 * P : (b0 + nb) * 4 * P].bitcast(F32).rearrange("p (b j u) -> p b j u", b=nb, u=2)
+            copy(on_vector, dst, backs[j0, b0][:].rearrange("p b u j -> p b j u"))
+
+        z_q = {}
+
+        def quantise_z(j0, j1):
+            codes = sbuf(f"z_cd{j0}", [P, j1 - j0], U32)
+            scales = sbuf(f"z_sc{j0}", [P, j1 - j0], U8)
+            nc.vector.quantize_mx(out=codes[:].bitcast(FP8X4), scales=scales[:], in_=z_grp[j0][:])
+            z_q[j0] = codes, scales
+
+        res = {}
+
+        def second_product(j0, j1, bank):
+            res[j0] = psum.tile([P, j1 - j0], F32, name="res", tag=f"bank{bank}")
             nc.tensor.matmul_mx(
-                out=res[:], lhsT=w2_cd[:].bitcast(FP4X4), lhsT_scale=w2_sc[:],
-                rhs=codes[:].bitcast(FP8X4), rhs_scale=scales[:], start=True, stop=True,
+                out=res[j0][:], lhsT=w2_cd[:].bitcast(FP4X4), lhsT_scale=w2_sc[:],
+                rhs=z_q[j0][0][:].bitcast(FP8X4), rhs_scale=z_q[j0][1][:], start=True, stop=True,
             )
-            res_sb = keep.tile([P, n], F32, name=f"res_sb{j0}")
-            if out_on_vector:
-                nc.vector.tensor_copy(res_sb[:], res[:])
-            else:
-                nc.scalar.copy(res_sb[:], res[:])
+
+        def store(j0, j1, on_vector):
+            res_sb = sbuf(f"res_sb{j0}", [P, j1 - j0], F32)
+            copy(on_vector, res_sb[:], res[j0][:])
             nc.sync.dma_start(out[:, j0:j1], res_sb[:])
 
-        quantise_w1(0)
-        first_layer(0)
-        quantise_w1(1)
-        quantise_w1(2)
-        first_layer(1)
-        quantise_w1(3)
-        first_layer(2)
-        first_layer(3)
-        influence(0, 0, 512)
-        influence(0, 512, 1024)
-        influence(1, 0, 512)
-        influence(1, 512, 1024)
-        influence(2, 0, 512)
-        influence(3, 0, 512)
-        second_layer(0, 256, False, False)
-        second_layer(256, 512, False, False)
-        influence(3, 512, 768)
-        influence(3, 768, 1024)
-        influence(2, 512, 768)
-        influence(2, 768, 1024)
-        second_layer(512, 768, True, False)
-        second_layer(768, 1024, True, True)
+        def warm(bank):
+            spare = psum.tile([P, HALF], F32, name="spare", tag=f"bank{bank}")
+            for z in range(PASSES):
+                nc.tensor.matmul_mx(
+                    out=spare[:], lhsT=w_q[0, z][0].bitcast(FP8X4), lhsT_scale=w_q[0, z][1],
+                    rhs=xw[z, 0].bitcast(FP8X4), rhs_scale=xs[4 * z : P, 0:HALF],
+                    start=(z == 0), stop=(z == PASSES - 1),
+                )
+
+        nc.vector.tensor_copy(xs[:], xs_all[:].indirect(offs_sb[:]))
+        pick_words(0, 0, 2)
+        pick_words(1, 0, 1)
+        round_w1(0, 0, False)
+        round_w1(0, 1, False)
+        quantise_w1(0, 0)
+        pick_words(1, 1, 2)
+        quantise_w1(0, 1)
+        round_w1(1, 0, True)
+        round_w1(1, 1, True)
+        quantise_w1(1, 0)
+        product(0, 0, 0, 0)
+        product(0, 0, 1, 1)
+        product(0, 1, 0)
+        product(0, 1, 1)
+        relu(0, 0)
+        relu(0, 1, True)
+        round_w1(2, 0, False)
+        round_w1(2, 1, False)
+        quantise_w1(2, 0)
+        product(1, 0, 0, 2)
+        product(1, 1, 0)
+        product(1, 0, 1, 3)
+        product(1, 1, 1)
+        relu(1, 0)
+        relu(1, 1)
+        round_w1(3, 0, False)
+        round_w1(3, 1, False)
+        quantise_w1(3, 0)
+        turn_h(0, 0, 512, 4)
+        turn_h(0, 512, 1024, 5)
+        product(2, 0, 0, 0)
+        product(2, 1, 0)
+        product(2, 0, 1, 1)
+        product(2, 1, 1)
+        relu(2, 0)
+        relu(2, 1)
+        gather(0, 0, 512)
+        turn_taken(0, 0, 512)
+        gather(0, 512, 1024)
+        turn_h(1, 0, 512, 6)
+        turn_h(1, 512, 1024, 7)
+        turn_taken(0, 512, 1024)
+        product(3, 0, 0, 2)
+        product(3, 1, 0)
+        product(3, 0, 1, 3)
+        product(3, 1, 1)
+        relu(3, 0)
+        relu(3, 1)
+        round_z(0, 0, 512)
+        round_z(0, 512, 1024)
+        gather(1, 0, 512)
+        turn_taken(1, 0, 512)
+        round_z(1, 0, 512)
+        gather(1, 512, 1024)
+        turn_h(2, 0, 512, 0)
+        turn_taken(1, 512, 1024)
+        gather(2, 0, 512)
+        turn_h(3, 0, 512, 1)
+        turn_taken(2, 0, 512)
+        round_z(2, 0, 512)
+        gather(3, 0, 512)
+        turn_h(3, 512, 1024, 2)
+        turn_taken(3, 0, 512)
+        turn_h(2, 512, 1024, 3)
+        round_z(3, 0, 512)
+        round_z(1, 512, 1024)
+        gather(3, 512, 1024)
+        turn_taken(3, 512, 1024)
+        turn_back(0, 512, 0, 2, 5)
+        turn_back(0, 512, 2, 2, 4)
+        weave(0, 512, 0, 2, False)
+        round_z(3, 512, 1024, False)
+        weave(0, 512, 2, 2, True)
+        gather(2, 512, 768)
+        gather(2, 768, 1024)
+        turn_taken(2, 512, 768)
+        turn_taken(2, 768, 1024)
+        quantise_z(0, 512)
+        round_z(2, 512, 1024, False)
+        turn_back(512, 768, 0, 2, 6)
+        turn_back(768, 1024, 0, 2, 0)
+        second_product(0, 512, 7)
+        weave(512, 768, 0, 2, True)
+        weave(768, 1024, 0, 2, False)
+        store(0, 512, False)
+        quantise_z(512, 768)
+        quantise_z(768, 1024)
+        second_product(512, 768, 5)
+        second_product(768, 1024, 2)
+        store(512, 768, True)
+        store(768, 1024, False)

@@ -30,9 +30,9 @@ def tile_picked_treeup_relu_p_kernel(
     with ExitStack() as ctx:
         keep = ctx.enter_context(tc.tile_pool(name="keep", bufs=1))
         psum = ctx.enter_context(tc.psum_pool(name="psum", bufs=1))
-        reuses = {"xw1_1":"w_raw0_0","w_grp1_0":"w_raw0_1","w_grp2_0":"w_cd0_1","taken0_512":"w_raw2_1","taken1_512":"w_raw3_1","z_t0":"w_raw3_0"}
+        reuses = {"xw1_1":"w_raw0_0","w_grp1_0":"w_raw0_1","w_grp2_0":"w_cd0_1","taken0_512":"w_raw2_1","taken1_512":"w_raw3_1","taken2_512":"taken3_0","taken2_768":"taken3_256","taken3_768":"taken3_512","taken3_896":"taken2_0"}
 
-        placed = {"xw_all0":0,"w_grp0_0":0,"w_grp0_1":1024,"z_t512":8192,"z_t768":10240,"w_grp3_0":9216,"w_cd1_0":9216,"taken3_0":12288,"taken2_512":12288,"taken2_768":13312}
+        placed = {"xw_all0":0,"w_grp0_0":0,"w_grp0_1":1024,"z_t512":8192,"z_t768":10240,"w_grp3_0":9728,"w_cd1_0":9728,"z_t0":12288,"z_t256":14336,"w_raw3_0":13312,"z_t896":11264}
         reuse = ctx.enter_context(tc.tile_pool(name="reuse", bufs=1))
 
         def sbuf(name, shape, dtype):
@@ -145,7 +145,7 @@ def tile_picked_treeup_relu_p_kernel(
             else:
                 nc.scalar.activation(h[c][:, cols], accs[c, b][:], ACT.Relu)
 
-        chunks = [(0,512), (512,768), (768,1024)]
+        chunks = [(0,256), (256,512), (512,768), (768,896), (896,1024)]
         z_t = {}
         for j0, j1 in chunks:
             z_t[j0] = sbuf(f"z_t{j0}", [P, (j1 - j0) // P, 2, P, 2], BF16)
@@ -189,6 +189,24 @@ def tile_picked_treeup_relu_p_kernel(
                         z_t[a0][:, :, :, 32 * c : 32 * (c + 1), :],
                         sums[c, j0][:, (a0 - j0) // P : (a1 - j0) // P, :].rearrange("j b (p u e) -> j b u p e", u=2, e=2),
                     )
+
+        pairs = {}
+
+        def turn_pair(source, c, j0, j1, first, last, bank=None, at=0):
+            if first:
+                pairs[j0] = psum.tile([P, (j1 - j0) // P, 2, P], F32, name="pair", tag=f"bank{bank}")
+            for b in range((j1 - j0) // P):
+                nc.tensor.matmul(
+                    pairs[j0][:, b, c - 2, :], source[:, at + b * P : at + (b + 1) * P], ident[:],
+                    start=(first and b == 0), stop=(last and b == (j1 - j0) // P - 1), is_transpose=True,
+                )
+
+        def round_pair(j0, on_vector=False):
+            copy(
+                on_vector,
+                z_t[j0][:, :, :, 64:128, :],
+                pairs[j0][:].rearrange("j b c (p u e) -> j b u (c p) e", u=2, e=2),
+            )
 
         z_grp = {}
         backs = {}
@@ -288,45 +306,68 @@ def tile_picked_treeup_relu_p_kernel(
         relu(3, 0)
         relu(3, 1)
         round_z(0, 0, 512)
-        round_z(0, 512, 1024)
         gather(1, 0, 512)
         turn_taken(1, 0, 512)
         round_z(1, 0, 512)
         gather(1, 512, 1024)
-        turn_h(2, 0, 512, 0)
+        turn_pair(h[2], 2, 0, 256, True, False, 0, 0)
+        turn_pair(h[2], 2, 256, 512, True, False, 1, 256)
         turn_taken(1, 512, 1024)
+        turn_pair(h[2], 2, 512, 768, True, False, 2, 512)
+        turn_pair(h[2], 2, 768, 896, True, False, 3, 768)
+        turn_pair(h[2], 2, 896, 1024, True, False, 4, 896)
         gather(2, 0, 512)
-        turn_h(3, 0, 512, 1)
-        turn_taken(2, 0, 512)
-        round_z(2, 0, 512)
-        gather(3, 0, 512)
-        turn_h(3, 512, 1024, 2)
-        turn_taken(3, 0, 512)
-        turn_h(2, 512, 1024, 3)
-        round_z(3, 0, 512)
+        turn_pair(h[3], 3, 0, 256, False, False, None, 0)
+        turn_pair(h[3], 3, 256, 512, False, False, None, 256)
+        turn_pair(taken[2, 0], 2, 0, 256, False, False, None, 0)
+        turn_pair(taken[2, 0], 2, 256, 512, False, False, None, 256)
+        turn_pair(h[3], 3, 512, 768, False, False, None, 512)
+        turn_pair(h[3], 3, 768, 896, False, False, None, 768)
+        turn_pair(h[3], 3, 896, 1024, False, False, None, 896)
+        round_z(0, 512, 1024)
         round_z(1, 512, 1024)
-        gather(3, 512, 1024)
-        turn_taken(3, 512, 1024)
-        turn_back(0, 512, 0, 2, 5)
-        turn_back(0, 512, 2, 2, 4)
-        weave(0, 512, 0, 2, False)
-        round_z(3, 512, 1024, False)
-        weave(0, 512, 2, 2, True)
+        gather(3, 0, 256)
+        gather(3, 256, 512)
+        turn_pair(taken[3, 0], 3, 0, 256, False, True)
+        round_pair(0)
+        turn_pair(taken[3, 256], 3, 256, 512, False, True)
+        turn_back(0, 256, 0, 2, 5)
+        round_pair(256)
+        weave(0, 256, 0, 2, False)
+        gather(3, 512, 768)
         gather(2, 512, 768)
+        turn_pair(taken[3, 512], 3, 512, 768, False, False)
+        turn_back(256, 512, 0, 2, 6)
+        turn_pair(taken[2, 512], 2, 512, 768, False, True)
+        round_pair(512)
         gather(2, 768, 1024)
-        turn_taken(2, 512, 768)
-        turn_taken(2, 768, 1024)
-        quantise_z(0, 512)
-        round_z(2, 512, 1024, False)
-        turn_back(512, 768, 0, 2, 6)
-        turn_back(768, 1024, 0, 2, 0)
-        second_product(0, 512, 7)
-        weave(512, 768, 0, 2, True)
-        weave(768, 1024, 0, 2, False)
-        store(0, 512, False)
+        gather(3, 768, 896)
+        gather(3, 896, 1024)
+        turn_pair(taken[2, 768], 2, 768, 896, False, False, None, 0)
+        turn_pair(taken[2, 768], 2, 896, 1024, False, False, None, 128)
+        turn_pair(taken[3, 768], 3, 768, 896, False, True)
+        turn_pair(taken[3, 896], 3, 896, 1024, False, True)
+        round_pair(768, False)
+        round_pair(896, True)
+        weave(256, 512, 0, 2, True)
+        quantise_z(0, 256)
+        turn_back(512, 768, 0, 2, 7)
+        turn_back(768, 896, 0, 1, 0)
+        turn_back(896, 1024, 0, 1, 1)
+        quantise_z(256, 512)
+        weave(512, 768, 0, 2, False)
+        weave(768, 896, 0, 1, True)
+        weave(896, 1024, 0, 1, False)
+        second_product(0, 256, 2)
+        second_product(256, 512, 3)
+        quantise_z(768, 896)
+        quantise_z(896, 1024)
         quantise_z(512, 768)
-        quantise_z(768, 1024)
-        second_product(512, 768, 5)
-        second_product(768, 1024, 2)
-        store(512, 768, True)
-        store(768, 1024, False)
+        store(0, 256, False)
+        store(256, 512, False)
+        second_product(768, 896, 5)
+        second_product(896, 1024, 6)
+        second_product(512, 768, 4)
+        store(768, 896, True)
+        store(896, 1024, True)
+        store(512, 768, False)

from contextlib import ExitStack

import concourse.mybir as mybir
from concourse.masks import make_identity

K, T, S, H, N = 1024, 2048, 1024, 512, 128
FLOPS = 2 * K * H * S + 2 * H * N * S

F32 = mybir.dt.float32
BF16 = mybir.dt.bfloat16
I32 = mybir.dt.int32
U32 = mybir.dt.uint32
U16 = mybir.dt.uint16
U8 = mybir.dt.uint8
FP8X4 = mybir.dt.float8_e4m3fn_x4
FP4X4 = mybir.dt.float4_e2m1fn_x4
ACT = mybir.ActivationFunctionType
MULT = mybir.AluOpType.mult

P = 128
PASSES = K // 512
HALF = 512
TILES = H // P


def tile_picked_treeup_relu_p_kernel(
    tc, x_words, x_scales, w1, w2_words, w2_scales, share, offs, par, out
):
    nc = tc.nc
    with ExitStack() as ctx:
        keep = ctx.enter_context(tc.tile_pool(name="keep", bufs=1))
        psum = ctx.enter_context(tc.psum_pool(name="psum", bufs=1))
        reuses = {"xw1_1":"w_raw0_0","w_grp1_0":"w_raw0_1","w_grp2_0":"w_cd0_1","taken0_512":"w_raw2_1","taken1_512":"w_raw3_1","taken2_512":"taken3_0","taken2_768":"taken3_256","taken3_768":"taken3_512","taken3_896":"taken2_0"}

        placed = {"xw_all0":0,"w_grp0_0":0,"w_grp0_1":1024,"z_t512":8192,"z_t768":10240,"w_grp3_0":9728,"w_cd1_0":9728,"z_t0":12288,"z_t256":14336,"w_raw3_0":13312,"z_t896":11264}
        reuse = ctx.enter_context(tc.tile_pool(name="reuse", bufs=1))

        def sbuf(name, shape, dtype):
            if name in placed:
                return reuse.tile(shape, dtype, name=name, offset=placed[name], align_bytes=64)
            return keep.tile(shape, dtype, name=name, tag=reuses.get(name, name), align_bytes=64)

        offs_sb = keep.tile([P, S // 16], U16, name="offs_sb")
        par_sb = keep.tile([P, S // 16], U16, name="par_sb")
        xs_all = sbuf("xs_all", [P, T], U8)
        w2_sc = sbuf("w2_sc", [P, N], U8)
        w2_cd = sbuf("w2_cd", [P, 2 * N], U8)
        nc.gpsimd.memset(xs_all[:].bitcast(I32), 0)
        nc.vector.memset(w2_sc[:].bitcast(I32), 0)
        ident = sbuf("ident", [P, P], F32)
        make_identity(nc, ident[:])

        share_col = sbuf("share_col", [P, 2, 4], F32)
        nc.sync.dma_start(offs_sb[:], offs)
        nc.sync.dma_start(par_sb[:], par)
        nc.scalar.dma_start(share_col[:], share[0, :].rearrange("(b p a) -> p b a", b=2, a=4))
        for q in range(4):
            nc.sync.dma_start(
                xs_all[32 * q : 32 * q + 8, :].bitcast(I32),
                x_scales[:, 4 * q : 4 * q + 4, :].bitcast(I32),
            )
        xw_all = []
        for z in range(PASSES):
            xw_all.append(sbuf(f"xw_all{z}", [P, T], I32))
            nc.sync.dma_start(xw_all[z][:], x_words[z].rearrange("p n t -> p (n t)").bitcast(I32))
        w_raw = {}
        for z, c0, c1 in [(0, 0, 1), (1, 0, 1), (0, 1, 2), (1, 1, 2), (0, 2, 3), (1, 2, 3), (0, 3, 4), (1, 3, 4)]:
            t = sbuf(f"w_raw{c0}_{z}", [P, 4, (c1 - c0) * P], F32)
            nc.sync.dma_start(
                t[:], w1[512 * z : 512 * (z + 1), c0 * P : c1 * P].rearrange("(p j) c -> p j c", j=4)
            )
            for c in range(c0, c1):
                w_raw[c, z] = t[:, :, (c - c0) * P : (c - c0 + 1) * P]
        nc.sync.dma_start(w2_cd[:].bitcast(I32), w2_words[0].bitcast(I32))
        for q in range(4):
            nc.sync.dma_start(
                w2_sc[32 * q : 32 * q + 4, :].bitcast(I32), w2_scales[0, 4 * q : 4 * q + 4, :].bitcast(I32)
            )

        share_sb = sbuf("share_sb", [P, S], F32)
        for b in range(2):
            bank = psum.tile([P, 4, P], F32, name="spread", tag=f"bank{6 + b}")
            for a in range(4):
                nc.tensor.transpose(bank[:, a, :], share_col[:, b, a : a + 1].to_broadcast([P, P]), ident[:])
            nc.scalar.activation(
                share_sb[:, HALF * b : HALF * (b + 1)].rearrange("p (n a) -> p n a", a=4),
                bank[:].rearrange("p a n -> p n a"),
                ACT.Copy,
            )

        xs = sbuf("xs", [P, S], U8)
        xw = {}
        w_q = {}
        h = [sbuf(f"h{c}", [P, S], F32) for c in range(TILES)]

        def pick_words(z, b0, b1):
            t = sbuf(f"xw{z}_{b0}", [P, HALF * (b1 - b0)], U32)
            nc.vector.tensor_copy(t[:], xw_all[z][:].bitcast(U32).indirect(offs_sb[:, 32 * b0 : 32 * b1]))
            for b in range(b0, b1):
                xw[z, b] = t[:, HALF * (b - b0) : HALF * (b - b0 + 1)]

        w_grp = {}

        def round_w1(c, z, on_vector):
            z0 = z if c == 0 else 0
            if z == z0:
                w_grp[c, z0] = sbuf(f"w_grp{c}_{z0}", [P, 1 if c == 0 else PASSES, P, 4], BF16)
            dst = w_grp[c, z0][:, z - z0, :, :].rearrange("p (c i) t -> p c t i", i=4)
            src = w_raw[c, z].rearrange("p t (c i) -> p c t i", i=4)
            if on_vector:
                nc.vector.tensor_copy(dst, src)
            else:
                nc.scalar.copy(dst, src)

        def quantise_w1(c, z0):
            passes = 1 if c == 0 else PASSES
            codes = sbuf(f"w_cd{c}_{z0}", [P, passes * P], U32)
            scales = sbuf(f"w_sc{c}_{z0}", [P, passes * P], U8)
            nc.vector.quantize_mx(
                out=codes[:].bitcast(FP8X4), scales=scales[:], in_=w_grp[c, z0][:].rearrange("p z c t -> p (z c t)")
            )
            for z in range(passes):
                w_q[c, z0 + z] = codes[:, z * P : (z + 1) * P], scales[:, z * P : (z + 1) * P]

        accs = {}

        def product(c, z, b, bank=None):
            if z == 0:
                accs[c, b] = psum.tile([P, HALF], F32, name="acc", tag=f"bank{bank}")
            cols = slice(HALF * b, HALF * (b + 1))
            nc.tensor.matmul_mx(
                out=accs[c, b][:],
                lhsT=w_q[c, z][0].bitcast(FP8X4),
                lhsT_scale=w_q[c, z][1],
                rhs=xw[z, b].bitcast(FP8X4),
                rhs_scale=xs[4 * z : P, cols],
                start=(z == 0),
                stop=(z == PASSES - 1),
            )

        def relu(c, b, on_vector=False):
            cols = slice(HALF * b, HALF * (b + 1))
            if on_vector:
                nc.vector.tensor_scalar(h[c][:, cols], accs[c, b][:], 0.0, None, op0=mybir.AluOpType.max)
            else:
                nc.scalar.activation(h[c][:, cols], accs[c, b][:], ACT.Relu)

        chunks = [(0,256), (256,512), (512,768), (768,896), (896,1024)]
        z_t = {}
        for j0, j1 in chunks:
            z_t[j0] = sbuf(f"z_t{j0}", [P, (j1 - j0) // P, 2, P, 2], BF16)

        taken = {}
        sums = {}

        def copy(on_vector, dst, src):
            if on_vector:
                nc.vector.tensor_copy(dst, src)
            else:
                nc.scalar.copy(dst, src)

        def gather(c, j0, j1):
            taken[c, j0] = sbuf(f"taken{c}_{j0}", [P, j1 - j0], F32)
            nc.vector.tensor_tensor(
                taken[c, j0][:], h[c][:].indirect(par_sb[:, j0 // 16 : j1 // 16]), share_sb[:, j0:j1], MULT
            )

        def turn_h(c, j0, j1, bank):
            sums[c, j0] = psum.tile([P, (j1 - j0) // P, P], F32, name="sums", tag=f"bank{bank}")
            for b in range((j1 - j0) // P):
                nc.tensor.matmul(
                    sums[c, j0][:, b, :], h[c][:, j0 + b * P : j0 + (b + 1) * P], ident[:],
                    start=(b == 0), stop=False, is_transpose=True,
                )

        def turn_taken(c, j0, j1):
            h0 = j0 // HALF * HALF
            for b in range((j1 - j0) // P):
                nc.tensor.matmul(
                    sums[c, h0][:, (j0 - h0) // P + b, :], taken[c, j0][:, b * P : (b + 1) * P], ident[:],
                    start=False, stop=(j0 + (b + 1) * P == h0 + HALF), is_transpose=True,
                )

        def round_z(c, j0, j1, on_vector=False):
            for a0, a1 in chunks:
                if j0 <= a0 and a1 <= j1:
                    copy(
                        on_vector,
                        z_t[a0][:, :, :, 32 * c : 32 * (c + 1), :],
                        sums[c, j0][:, (a0 - j0) // P : (a1 - j0) // P, :].rearrange("j b (p u e) -> j b u p e", u=2, e=2),
                    )

        pairs = {}

        def turn_pair(source, c, j0, j1, first, last, bank=None, at=0):
            if first:
                pairs[j0] = psum.tile([P, (j1 - j0) // P, 2, P], F32, name="pair", tag=f"bank{bank}")
            for b in range((j1 - j0) // P):
                nc.tensor.matmul(
                    pairs[j0][:, b, c - 2, :], source[:, at + b * P : at + (b + 1) * P], ident[:],
                    start=(first and b == 0), stop=(last and b == (j1 - j0) // P - 1), is_transpose=True,
                )

        def round_pair(j0, on_vector=False):
            copy(
                on_vector,
                z_t[j0][:, :, :, 64:128, :],
                pairs[j0][:].rearrange("j b c (p u e) -> j b u (c p) e", u=2, e=2),
            )

        z_grp = {}
        backs = {}

        def turn_back(j0, j1, b0, nb, bank):
            words = z_t[j0][:].rearrange("j b u p e -> j (b u p e)").bitcast(F32)
            backs[j0, b0] = psum.tile([P, nb, 2, P], F32, name="back", tag=f"bank{bank}")
            for b in range(nb):
                for u in range(2):
                    w0 = ((b0 + b) * 2 + u) * P
                    nc.tensor.transpose(backs[j0, b0][:, b, u, :], words[:, w0 : w0 + P], ident[:])

        def weave(j0, j1, b0, nb, on_vector):
            if b0 == 0:
                z_grp[j0] = sbuf(f"z_grp{j0}", [P, (j1 - j0) * 4], BF16)
            dst = z_grp[j0][:, b0 * 4 * P : (b0 + nb) * 4 * P].bitcast(F32).rearrange("p (b j u) -> p b j u", b=nb, u=2)
            copy(on_vector, dst, backs[j0, b0][:].rearrange("p b u j -> p b j u"))

        z_q = {}

        def quantise_z(j0, j1):
            codes = sbuf(f"z_cd{j0}", [P, j1 - j0], U32)
            scales = sbuf(f"z_sc{j0}", [P, j1 - j0], U8)
            nc.vector.quantize_mx(out=codes[:].bitcast(FP8X4), scales=scales[:], in_=z_grp[j0][:])
            z_q[j0] = codes, scales

        res = {}

        def second_product(j0, j1, bank):
            res[j0] = psum.tile([P, j1 - j0], F32, name="res", tag=f"bank{bank}")
            nc.tensor.matmul_mx(
                out=res[j0][:], lhsT=w2_cd[:].bitcast(FP4X4), lhsT_scale=w2_sc[:],
                rhs=z_q[j0][0][:].bitcast(FP8X4), rhs_scale=z_q[j0][1][:], start=True, stop=True,
            )

        def store(j0, j1, on_vector):
            res_sb = sbuf(f"res_sb{j0}", [P, j1 - j0], F32)
            copy(on_vector, res_sb[:], res[j0][:])
            nc.sync.dma_start(out[:, j0:j1], res_sb[:])

        def warm(bank):
            spare = psum.tile([P, HALF], F32, name="spare", tag=f"bank{bank}")
            for z in range(PASSES):
                nc.tensor.matmul_mx(
                    out=spare[:], lhsT=w_q[0, z][0].bitcast(FP8X4), lhsT_scale=w_q[0, z][1],
                    rhs=xw[z, 0].bitcast(FP8X4), rhs_scale=xs[4 * z : P, 0:HALF],
                    start=(z == 0), stop=(z == PASSES - 1),
                )

        nc.vector.tensor_copy(xs[:], xs_all[:].indirect(offs_sb[:]))
        pick_words(0, 0, 2)
        pick_words(1, 0, 1)
        round_w1(0, 0, False)
        round_w1(0, 1, False)
        quantise_w1(0, 0)
        pick_words(1, 1, 2)
        quantise_w1(0, 1)
        round_w1(1, 0, True)
        round_w1(1, 1, True)
        quantise_w1(1, 0)
        product(0, 0, 0, 0)
        product(0, 0, 1, 1)
        product(0, 1, 0)
        product(0, 1, 1)
        relu(0, 0)
        relu(0, 1, True)
        round_w1(2, 0, False)
        round_w1(2, 1, False)
        quantise_w1(2, 0)
        product(1, 0, 0, 2)
        product(1, 1, 0)
        product(1, 0, 1, 3)
        product(1, 1, 1)
        relu(1, 0)
        relu(1, 1)
        round_w1(3, 0, False)
        round_w1(3, 1, False)
        quantise_w1(3, 0)
        turn_h(0, 0, 512, 4)
        turn_h(0, 512, 1024, 5)
        product(2, 0, 0, 0)
        product(2, 1, 0)
        product(2, 0, 1, 1)
        product(2, 1, 1)
        relu(2, 0)
        relu(2, 1)
        gather(0, 0, 512)
        turn_taken(0, 0, 512)
        gather(0, 512, 1024)
        turn_h(1, 0, 512, 6)
        turn_h(1, 512, 1024, 7)
        turn_taken(0, 512, 1024)
        product(3, 0, 0, 2)
        product(3, 1, 0)
        product(3, 0, 1, 3)
        product(3, 1, 1)
        relu(3, 0)
        relu(3, 1)
        round_z(0, 0, 512)
        gather(1, 0, 512)
        turn_taken(1, 0, 512)
        round_z(1, 0, 512)
        gather(1, 512, 1024)
        turn_pair(h[2], 2, 0, 256, True, False, 0, 0)
        turn_pair(h[2], 2, 256, 512, True, False, 1, 256)
        turn_taken(1, 512, 1024)
        turn_pair(h[2], 2, 512, 768, True, False, 2, 512)
        turn_pair(h[2], 2, 768, 896, True, False, 3, 768)
        turn_pair(h[2], 2, 896, 1024, True, False, 4, 896)
        gather(2, 0, 512)
        turn_pair(h[3], 3, 0, 256, False, False, None, 0)
        turn_pair(h[3], 3, 256, 512, False, False, None, 256)
        turn_pair(taken[2, 0], 2, 0, 256, False, False, None, 0)
        turn_pair(taken[2, 0], 2, 256, 512, False, False, None, 256)
        turn_pair(h[3], 3, 512, 768, False, False, None, 512)
        turn_pair(h[3], 3, 768, 896, False, False, None, 768)
        turn_pair(h[3], 3, 896, 1024, False, False, None, 896)
        round_z(0, 512, 1024)
        round_z(1, 512, 1024)
        gather(3, 0, 256)
        gather(3, 256, 512)
        turn_pair(taken[3, 0], 3, 0, 256, False, True)
        round_pair(0)
        turn_pair(taken[3, 256], 3, 256, 512, False, True)
        turn_back(0, 256, 0, 2, 5)
        round_pair(256)
        weave(0, 256, 0, 2, False)
        gather(3, 512, 768)
        gather(2, 512, 768)
        turn_pair(taken[3, 512], 3, 512, 768, False, False)
        turn_back(256, 512, 0, 2, 6)
        turn_pair(taken[2, 512], 2, 512, 768, False, True)
        round_pair(512)
        gather(2, 768, 1024)
        gather(3, 768, 896)
        gather(3, 896, 1024)
        turn_pair(taken[2, 768], 2, 768, 896, False, False, None, 0)
        turn_pair(taken[2, 768], 2, 896, 1024, False, False, None, 128)
        turn_pair(taken[3, 768], 3, 768, 896, False, True)
        turn_pair(taken[3, 896], 3, 896, 1024, False, True)
        round_pair(768, False)
        round_pair(896, True)
        weave(256, 512, 0, 2, True)
        quantise_z(0, 256)
        turn_back(512, 768, 0, 2, 7)
        turn_back(768, 896, 0, 1, 0)
        turn_back(896, 1024, 0, 1, 1)
        quantise_z(256, 512)
        weave(512, 768, 0, 2, False)
        weave(768, 896, 0, 1, True)
        weave(896, 1024, 0, 1, False)
        second_product(0, 256, 2)
        second_product(256, 512, 3)
        quantise_z(768, 896)
        quantise_z(896, 1024)
        quantise_z(512, 768)
        store(0, 256, False)
        store(256, 512, False)
        second_product(768, 896, 5)
        second_product(896, 1024, 6)
        second_product(512, 768, 4)
        store(768, 896, True)
        store(896, 1024, True)
        store(512, 768, False)
